import numpy as np
import ml_dtypes


def mxq(x, axis, fmt="e4m3"):
    dtype, down = {"e4m3": (ml_dtypes.float8_e4m3fn, 7), "e5m2": (ml_dtypes.float8_e5m2, 14)}[fmt]
    v = np.moveaxis(np.asarray(x, np.float32).astype(ml_dtypes.bfloat16).astype(np.float64), axis, -1)
    blocks = v.reshape(v.shape[:-1] + (-1, 32))
    amax = np.abs(blocks).max(-1, keepdims=True)
    byte = np.maximum(np.where(amax > 0, np.frexp(amax)[1] - 1 + 127, 0) - down, 1)
    scale = np.exp2(byte - 127.0)
    codes = (blocks / scale).astype(np.float32).astype(dtype).astype(np.float64)
    return np.moveaxis((codes * scale).reshape(v.shape), -1, axis)


WIDE = False


def mx_kscale(k):
    if not WIDE:
        return np.ones(k)
    levels = np.array([10, -10, 5, -5, 0])
    if k % 512:
        return np.exp2(np.random.permutation(np.resize(levels, k // 32))).repeat(32)
    a = np.empty((k // 512, 16))
    for p in range(k // 512):
        a[p, :8] = np.random.permutation(np.resize(levels, 8))
        for g in range(8):
            far = levels[np.abs(levels - a[p, g]) >= 10]
            a[p, g + 8] = far[np.random.randint(len(far))]
    return np.exp2(a.ravel()).repeat(32)


def f64(x):
    return np.asarray(x).astype(np.float64)


def striped(idx):
    return np.tile(np.asarray(idx).reshape(-1, 16).T, (8, 1)).astype(np.uint16)


def unstriped(offs):
    return offs[:16].T.reshape(-1).astype(np.int64)


def bf(x):
    return np.asarray(x, np.float32).astype(ml_dtypes.bfloat16)


def planes(Y):
    r, m = Y.shape
    b = f64(bf(Y)).reshape(r // 32, 32, m)
    amax = np.abs(b).max(1)
    byte = np.clip(np.where(amax > 0, np.frexp(amax)[1] - 1 + 127 - 7, 1), 1, 254)
    codes = (b * np.exp2(127.0 - byte)[:, None, :]).reshape(r, m).astype(np.float32).astype(ml_dtypes.float8_e4m3fn).view(np.uint8)
    words = codes.reshape(r // 512, 128, 4, m).transpose(0, 1, 3, 2)
    return np.ascontiguousarray(words), np.ascontiguousarray(byte.astype(np.uint8).reshape(r // 512, 16, m))


E, T, I, J, F = 512, 2048, 512, 512, 512


def setup_inputs():
    n = np.random.standard_normal
    idx = np.random.permutation(T)[:I]
    fe = mx_kscale(E)
    fi = mx_kscale(I)
    ti = np.ones(T)
    ti[idx] = fi
    return {
        "tok": (n((E, T)) / fe[:, None] / ti).astype(np.float32),
        "ci": ((np.cos(2 * np.pi * np.arange(I)[:, None] * np.arange(J) / I) / np.sqrt(I)) * fi[:, None]).astype(np.float32),
        "si": ((np.sin(2 * np.pi * np.arange(I)[:, None] * np.arange(J) / I) / np.sqrt(I)) * fi[:, None]).astype(np.float32),
        "ce": ((2.0 * np.cos(2 * np.pi * np.arange(E)[:, None] * np.arange(F) / E) / np.sqrt(E)) * fe[:, None]).astype(np.float32),
        "se": ((-2.0 * np.sin(2 * np.pi * np.arange(E)[:, None] * np.arange(F) / E) / np.sqrt(E)) * fe[:, None]).astype(np.float32),
        "offs": striped(idx),
    }


def reference(tok, ci, si, ce, se, offs):
    idx = unstriped(offs)
    xt = f64(tok)[:, idx].T
    ciq = mxq(f64(ci), 0, "e4m3")
    xtq = mxq(xt, 0, "e4m3")
    a = ciq.T @ xtq
    siq = mxq(f64(si), 0, "e4m3")
    b = siq.T @ xtq
    at = a.T
    bt = b.T
    ceq = mxq(f64(ce), 0, "e4m3")
    atq = mxq(at, 0, "e4m3")
    seq = mxq(f64(se), 0, "e4m3")
    btq = mxq(bt, 0, "e4m3")
    y = ceq.T @ atq + seq.T @ btq
    words, scales = planes(y)
    return y, words, scales

@@ -1,0 +1,200 @@
+from contextlib import ExitStack
+
+import concourse.mybir as mybir
+from concourse.masks import make_identity
+
+E, T, I, J, F = 512, 2048, 512, 512, 512
+FLOPS = 4 * 2 * 512 * 512 * 512
+
+F32 = mybir.dt.float32
+BF16 = mybir.dt.bfloat16
+I32 = mybir.dt.int32
+U32 = mybir.dt.uint32
+U16 = mybir.dt.uint16
+U8 = mybir.dt.uint8
+FP8X4 = mybir.dt.float8_e4m3fn_x4
+
+P = 128
+PACK = 4
+BLK = 128
+HALF = 256
+
+
+def tile_attend_fouriermix_pl_kernel(tc, tok, ci, si, ce, se, offs, out_0, out_1, out_2):
+    nc = tc.nc
+    with ExitStack() as ctx:
+        keep = ctx.enter_context(tc.tile_pool(name="keep", bufs=1))
+        psum = ctx.enter_context(tc.psum_pool(name="psum", bufs=1))
+
+        def sb(shape, dtype, name, tag=None):
+            return keep.tile(shape, dtype, name=name, tag=tag or name, align_bytes=64)
+
+        def bank(b, shape, name):
+            return psum.tile(shape, F32, name=name, tag=f"bank{b}")
+
+        def quantize(codes, scales, values):
+            nc.vector.quantize_mx(out=codes.bitcast(FP8X4), scales=scales, in_=values)
+
+        def matmul(out, w_codes, w_scales, m_codes, m_scales, start, stop):
+            nc.tensor.matmul_mx(out=out, lhsT=w_codes.bitcast(FP8X4), lhsT_scale=w_scales,
+                                rhs=m_codes.bitcast(FP8X4), rhs_scale=m_scales, start=start, stop=stop)
+
+        offsets = keep.tile([P, I // 16], U16, name="offsets")
+        tok_rows = tok.rearrange("(m t) c -> m t c", t=PACK)
+        planes = [sb([P, T], F32, f"tok{t}") for t in range(PACK)]
+        nc.sync.dma_start(planes[0][:], tok_rows[:, 0, :])
+        nc.sync.dma_start(offsets[:], offs)
+        for t in range(1, PACK):
+            nc.sync.dma_start(planes[t][:], tok_rows[:, t, :])
+        sources = {"ci": ci, "si": si, "ce": ce, "se": se}
+        raw = {}
+        for name, h in (("ci", 0), ("si", 0), ("ci", 1), ("si", 1), ("ce", 0), ("ce", 1), ("se", 0), ("se", 1)):
+            raw[name, h] = sb([P, PACK, HALF], F32, f"raw_{name}{h}")
+            rows = sources[name].rearrange("(p t) c -> p t c", t=PACK)
+            nc.sync.dma_start(raw[name, h][:], rows[:, :, h * HALF:(h + 1) * HALF])
+
+        ident = sb([P, P], F32, "ident")
+        make_identity(nc, ident[:])
+
+        x_vals = sb([P, PACK * I], BF16, "x_vals")
+        x_codes = {}
+        x_scales = sb([P, E], U8, "x_scales")
+
+        def quantize_tokens(h, tag):
+            x_codes[h] = sb([P, HALF], U32, f"x_codes{h}", tag)
+            quantize(x_codes[h][:], x_scales[:, h * HALF:(h + 1) * HALF],
+                     x_vals[:, h * PACK * HALF:(h + 1) * PACK * HALF])
+
+        def quantize_half(vals, codes, scales, h):
+            quantize(codes[:, h * HALF:(h + 1) * HALF], scales[:, h * HALF:(h + 1) * HALF],
+                     vals[:, h * PACK * HALF:(h + 1) * PACK * HALF])
+
+        for t in range(PACK):
+            picked = sb([P, I], BF16, f"picked{t}")
+            nc.vector.tensor_copy(picked[:], planes[t][:].indirect(offsets[:]))
+            pairs = picked[:].bitcast(F32)
+            turned = bank(6 + t % 2, [P, 2, P], f"turned{t}")
+            for u in range(2):
+                nc.tensor.transpose(turned[:, u, :], pairs[:, u:I // 2:2], ident[:])
+            nc.scalar.copy(x_vals[:, t * I:(t + 1) * I].bitcast(F32).rearrange("p (m u) -> p m u", u=2),
+                           turned[:].rearrange("p u m -> p m u"))
+            if t == 1:
+                quantize_tokens(0, None)
+
+        mixed = {}
+        for name in ("ci", "si"):
+            mixed[name] = (sb([P, PACK * J], BF16, f"{name}_out_vals"), sb([P, J], U32, f"{name}_out_codes"),
+                           sb([P, J], U8, f"{name}_out_scales"))
+
+        moving = {}
+
+        def prepare(name, h):
+            staged = sb([P, PACK * HALF], BF16, f"{name}_vals{h}")
+            nc.vector.tensor_copy(
+                staged[:].rearrange("p (c i t) -> p c t i", i=4, t=PACK),
+                raw[name, h][:].rearrange("p t (c i) -> p c t i", i=4))
+            w_codes = sb([P, HALF], U32, f"{name}_codes{h}")
+            w_scales = sb([P, HALF], U8, f"{name}_scales{h}")
+            quantize(w_codes[:], w_scales[:], staged[:])
+            for k in range(2):
+                moving[name, 2 * h + k] = (w_codes[:, k * BLK:(k + 1) * BLK], w_scales[:, k * BLK:(k + 1) * BLK])
+
+        def first_stage(name, h):
+            vals = mixed[name][0]
+            for b in (2 * h, 2 * h + 1):
+                w_codes, w_scales = moving[name, b]
+                acc = bank((0 if name == "ci" else 4) + b, [P, PACK, BLK], f"{name}_acc{b}")
+                for t in range(PACK):
+                    cols = slice(t * BLK, (t + 1) * BLK)
+                    matmul(acc[:, t, :], x_codes[t // 2][:, (t % 2) * BLK:(t % 2 + 1) * BLK], x_scales[:, cols], w_codes, w_scales, True, True)
+                nc.scalar.copy(
+                    vals[:, b * PACK * BLK:(b + 1) * PACK * BLK].rearrange("p (j t) -> p j t", t=PACK),
+                    acc[:].rearrange("p t j -> p j t"))
+
+        a_vals, a_codes, a_scales = mixed["ci"]
+        b_vals, b_codes, b_scales = mixed["si"]
+        prepare("ci", 0)
+        prepare("si", 0)
+        quantize_tokens(1, "raw_si0")
+        first_stage("ci", 0)
+        first_stage("si", 0)
+        prepare("ci", 1)
+        first_stage("ci", 1)
+        prepare("si", 1)
+        first_stage("si", 1)
+        quantize_half(a_vals, a_codes, a_scales, 0)
+
+        def deal(vals, name, h):
+            nc.vector.tensor_copy(
+                vals[:].rearrange("p (r m t) -> p m t r", r=PACK, t=PACK)[:, 64 * h:64 * h + 64],
+                raw[name, h][:].rearrange("p t (m r) -> p m t r", r=PACK))
+
+        ce_vals = sb([P, PACK * F], BF16, "ce_vals")
+        ce_codes = sb([P, F], U32, "ce_codes")
+        ce_scales = sb([P, F], U8, "ce_scales")
+        deal(ce_vals, "ce", 0)
+        quantize_half(b_vals, b_codes, b_scales, 0)
+        deal(ce_vals, "ce", 1)
+        quantize_half(a_vals, a_codes, a_scales, 1)
+        quantize_half(ce_vals, ce_codes, ce_scales, 0)
+        quantize_half(ce_vals, ce_codes, ce_scales, 1)
+
+        y_acc = {}
+        for h in range(2):
+            half = slice(h * HALF, (h + 1) * HALF)
+            for r in range(PACK):
+                cols = slice(r * BLK, (r + 1) * BLK)
+                y_acc[h, r] = bank(PACK * h + r, [P, HALF], f"y_acc{h}{r}")
+                matmul(y_acc[h, r][:], ce_codes[:, cols], ce_scales[:, cols], a_codes[:, half], a_scales[:, half], True, False)
+
+        se_vals = sb([P, PACK * F], BF16, "se_vals")
+        se_codes = sb([P, F], U32, "se_codes")
+        se_scales = sb([P, F], U8, "se_scales")
+        deal(se_vals, "se", 0)
+        quantize_half(b_vals, b_codes, b_scales, 1)
+        deal(se_vals, "se", 1)
+        for r in range(PACK):
+            cols = slice(r * BLK, (r + 1) * BLK)
+            quantize(se_codes[:, cols], se_scales[:, cols], se_vals[:, PACK * r * BLK:PACK * (r + 1) * BLK])
+
+        y = [sb([P, PACK, HALF], F32, f"y{h}") for h in range(2)]
+        y_rows = out_0.rearrange("(p r) j -> p r j", r=PACK)
+        y_vals = sb([P, PACK * J], BF16, "y_vals")
+        y_codes = sb([P, J], U32, "y_codes")
+        y_scales = sb([P, J], U8, "y_scales")
+        words = out_1[0].rearrange("l c r -> l (c r)").bitcast(I32)
+
+        def weave(engine_copy, j0, j1):
+            h = j0 // HALF
+            engine_copy(
+                y_vals[:, PACK * j0:PACK * j1].rearrange("p (c i r) -> p c r i", i=4, r=PACK),
+                y[h][:, :, j0 - h * HALF:j1 - h * HALF].rearrange("p r (c i) -> p c r i", i=4))
+
+        def quantize_result(j0, j1):
+            quantize(y_codes[:, j0:j1], y_scales[:, j0:j1], y_vals[:, PACK * j0:PACK * j1])
+
+        for h in range(2):
+            half = slice(h * HALF, (h + 1) * HALF)
+            for r in range(PACK):
+                cols = slice(r * BLK, (r + 1) * BLK)
+                matmul(y_acc[h, r][:], se_codes[:, cols], se_scales[:, cols], b_codes[:, half], b_scales[:, half], False, True)
+                if h == 0 and r % 2 == 1:
+                    nc.vector.tensor_copy(y[h][:, r, :], y_acc[h, r][:])
+                else:
+                    nc.scalar.copy(y[h][:, r, :], y_acc[h, r][:])
+                if r % 2 == 1:
+                    nc.sync.dma_start(y_rows[:, r - 1:r + 1, half], y[h][:, r - 1:r + 1, :])
+            if h == 0:
+                weave(nc.vector.tensor_copy, 0, HALF)
+                quantize_result(0, HALF)
+                nc.sync.dma_start(words[:, half], y_codes[:, half].bitcast(I32))
+            else:
+                weave(nc.vector.tensor_copy, HALF, HALF + BLK)
+                weave(nc.scalar.copy, HALF + BLK, J)
+                quantize_result(HALF, HALF + BLK)
+                quantize_result(HALF + BLK, J)
+                nc.sync.dma_start(words[:, half], y_codes[:, half].bitcast(I32))
+        scale_rows = out_2[0].bitcast(I32)
+        for q in range(4):
+            queue = nc.scalar if q % 2 == 0 else nc.sync
+            queue.dma_start(scale_rows[4 * q:4 * q + 4, :], y_scales[32 * q:32 * q + 4, :].bitcast(I32))

@@ -46,12 +46,10 @@ def tile_attend_fouriermix_pl_kernel(tc, tok, ci, si, ce, se, offs, out_0, out_1
         nc.sync.dma_start(offsets[:], offs)
         for t in range(1, PACK):
             nc.sync.dma_start(planes[t][:], tok_rows[:, t, :])
-        sources = {"ci": ci, "si": si, "ce": ce, "se": se}
         raw = {}
-        for name, h in (("ci", 0), ("si", 0), ("ci", 1), ("si", 1), ("ce", 0), ("ce", 1), ("se", 0), ("se", 1)):
-            raw[name, h] = sb([P, PACK, HALF], F32, f"raw_{name}{h}")
-            rows = sources[name].rearrange("(p t) c -> p t c", t=PACK)
-            nc.sync.dma_start(raw[name, h][:], rows[:, :, h * HALF:(h + 1) * HALF])
+        for name, src in (("ci", ci), ("si", si), ("ce", ce), ("se", se)):
+            raw[name] = sb([P, PACK, 512], F32, f"raw_{name}")
+            nc.sync.dma_start(raw[name][:], src.rearrange("(p t) c -> p t c", t=PACK))
 
         ident = sb([P, P], F32, "ident")
         make_identity(nc, ident[:])
@@ -60,14 +58,11 @@ def tile_attend_fouriermix_pl_kernel(tc, tok, ci, si, ce, se, offs, out_0, out_1
         x_codes = {}
         x_scales = sb([P, E], U8, "x_scales")
 
-        def quantize_tokens(h, tag):
-            x_codes[h] = sb([P, HALF], U32, f"x_codes{h}", tag)
-            quantize(x_codes[h][:], x_scales[:, h * HALF:(h + 1) * HALF],
-                     x_vals[:, h * PACK * HALF:(h + 1) * PACK * HALF])
-
-        def quantize_half(vals, codes, scales, h):
-            quantize(codes[:, h * HALF:(h + 1) * HALF], scales[:, h * HALF:(h + 1) * HALF],
-                     vals[:, h * PACK * HALF:(h + 1) * PACK * HALF])
+        def quantize_tokens(t0, t1, tag):
+            codes = sb([P, (t1 - t0) * BLK], U32, f"x_codes{t0}", tag)
+            quantize(codes[:], x_scales[:, t0 * BLK:t1 * BLK], x_vals[:, t0 * I:t1 * I])
+            for t in range(t0, t1):
+                x_codes[t] = codes[:, (t - t0) * BLK:(t - t0 + 1) * BLK]
 
         for t in range(PACK):
             picked = sb([P, I], BF16, f"picked{t}")
@@ -79,20 +74,28 @@ def tile_attend_fouriermix_pl_kernel(tc, tok, ci, si, ce, se, offs, out_0, out_1
             nc.scalar.copy(x_vals[:, t * I:(t + 1) * I].bitcast(F32).rearrange("p (m u) -> p m u", u=2),
                            turned[:].rearrange("p u m -> p m u"))
             if t == 1:
-                quantize_tokens(0, None)
+                quantize_tokens(0, 2, None)
+
+        quantize_tokens(2, 3, "tok3")
 
         mixed = {}
         for name in ("ci", "si"):
-            mixed[name] = (sb([P, PACK * J], BF16, f"{name}_out_vals"), sb([P, J], U32, f"{name}_out_codes"),
-                           sb([P, J], U8, f"{name}_out_scales"))
+            mixed[name] = (sb([P, PACK * J], BF16, f"{name}_out_vals"), sb([P, J], U8, f"{name}_out_scales"))
+        mixed_codes = {}
+
+        def quantize_mixed(name, h, tag):
+            vals, scales = mixed[name]
+            mixed_codes[name, h] = sb([P, HALF], U32, f"{name}_out_codes{h}", tag)
+            quantize(mixed_codes[name, h][:], scales[:, h * HALF:(h + 1) * HALF],
+                     vals[:, h * PACK * HALF:(h + 1) * PACK * HALF])
 
         moving = {}
 
-        def prepare(name, h):
+        def prepare(name, h, engine_copy):
             staged = sb([P, PACK * HALF], BF16, f"{name}_vals{h}")
-            nc.vector.tensor_copy(
+            engine_copy(
                 staged[:].rearrange("p (c i t) -> p c t i", i=4, t=PACK),
-                raw[name, h][:].rearrange("p t (c i) -> p c t i", i=4))
+                raw[name][:, :, h * HALF:(h + 1) * HALF].rearrange("p t (c i) -> p c t i", i=4))
             w_codes = sb([P, HALF], U32, f"{name}_codes{h}")
             w_scales = sb([P, HALF], U8, f"{name}_scales{h}")
             quantize(w_codes[:], w_scales[:], staged[:])
@@ -103,41 +106,35 @@ def tile_attend_fouriermix_pl_kernel(tc, tok, ci, si, ce, se, offs, out_0, out_1
             vals = mixed[name][0]
             for b in (2 * h, 2 * h + 1):
                 w_codes, w_scales = moving[name, b]
-                acc = bank((0 if name == "ci" else 4) + b, [P, PACK, BLK], f"{name}_acc{b}")
+                acc = bank((0 if name == "ci" else PACK) + b, [P, PACK, BLK], f"{name}_acc{b}")
                 for t in range(PACK):
                     cols = slice(t * BLK, (t + 1) * BLK)
-                    matmul(acc[:, t, :], x_codes[t // 2][:, (t % 2) * BLK:(t % 2 + 1) * BLK], x_scales[:, cols], w_codes, w_scales, True, True)
+                    matmul(acc[:, t, :], x_codes[t], x_scales[:, cols], w_codes, w_scales, True, True)
                 nc.scalar.copy(
                     vals[:, b * PACK * BLK:(b + 1) * PACK * BLK].rearrange("p (j t) -> p j t", t=PACK),
                     acc[:].rearrange("p t j -> p j t"))
 
-        a_vals, a_codes, a_scales = mixed["ci"]
-        b_vals, b_codes, b_scales = mixed["si"]
-        prepare("ci", 0)
-        prepare("si", 0)
-        quantize_tokens(1, "raw_si0")
+        a_scales = mixed["ci"][1]
+        b_scales = mixed["si"][1]
+        prepare("ci", 0, nc.vector.tensor_copy)
+        quantize_tokens(3, 4, "ci_vals0")
+        prepare("ci", 1, nc.scalar.copy)
         first_stage("ci", 0)
-        first_stage("si", 0)
-        prepare("ci", 1)
         first_stage("ci", 1)
-        prepare("si", 1)
+        prepare("si", 0, nc.vector.tensor_copy)
+        prepare("si", 1, nc.vector.tensor_copy)
+        first_stage("si", 0)
         first_stage("si", 1)
-        quantize_half(a_vals, a_codes, a_scales, 0)
-
-        def deal(vals, name, h):
-            nc.vector.tensor_copy(
-                vals[:].rearrange("p (r m t) -> p m t r", r=PACK, t=PACK)[:, 64 * h:64 * h + 64],
-                raw[name, h][:].rearrange("p t (m r) -> p m t r", r=PACK))
+        quantize_mixed("ci", 0, "si_vals0")
 
         ce_vals = sb([P, PACK * F], BF16, "ce_vals")
         ce_codes = sb([P, F], U32, "ce_codes")
         ce_scales = sb([P, F], U8, "ce_scales")
-        deal(ce_vals, "ce", 0)
-        quantize_half(b_vals, b_codes, b_scales, 0)
-        deal(ce_vals, "ce", 1)
-        quantize_half(a_vals, a_codes, a_scales, 1)
-        quantize_half(ce_vals, ce_codes, ce_scales, 0)
-        quantize_half(ce_vals, ce_codes, ce_scales, 1)
+        nc.vector.tensor_copy(ce_vals[:].rearrange("p (r m t) -> p m t r", r=PACK, t=PACK),
+                              raw["ce"][:].rearrange("p t (m r) -> p m t r", r=PACK))
+        quantize_mixed("ci", 1, "raw_ce")
+        quantize(ce_codes[:], ce_scales[:], ce_vals[:])
+        quantize_mixed("si", 0, "ce_vals")
 
         y_acc = {}
         for h in range(2):
@@ -145,17 +142,20 @@ def tile_attend_fouriermix_pl_kernel(tc, tok, ci, si, ce, se, offs, out_0, out_1
             for r in range(PACK):
                 cols = slice(r * BLK, (r + 1) * BLK)
                 y_acc[h, r] = bank(PACK * h + r, [P, HALF], f"y_acc{h}{r}")
-                matmul(y_acc[h, r][:], ce_codes[:, cols], ce_scales[:, cols], a_codes[:, half], a_scales[:, half], True, False)
+                matmul(y_acc[h, r][:], ce_codes[:, cols], ce_scales[:, cols], mixed_codes["ci", h][:], a_scales[:, half], True, False)
 
-        se_vals = sb([P, PACK * F], BF16, "se_vals")
         se_codes = sb([P, F], U32, "se_codes")
         se_scales = sb([P, F], U8, "se_scales")
-        deal(se_vals, "se", 0)
-        quantize_half(b_vals, b_codes, b_scales, 1)
-        deal(se_vals, "se", 1)
-        for r in range(PACK):
-            cols = slice(r * BLK, (r + 1) * BLK)
-            quantize(se_codes[:, cols], se_scales[:, cols], se_vals[:, PACK * r * BLK:PACK * (r + 1) * BLK])
+        for pair, engine_copy in ((0, nc.vector.tensor_copy), (1, nc.scalar.copy)):
+            se_vals = sb([P, 2 * BLK * PACK], BF16, f"se_vals{pair}")
+            engine_copy(
+                se_vals[:].rearrange("p (r m t) -> p m t r", r=2, t=PACK),
+                raw["se"][:].rearrange("p t (m r) -> p m t r", r=PACK)[:, :, :, 2 * pair:2 * pair + 2])
+            if pair == 1:
+                quantize_mixed("si", 1, "se_vals0")
+            for k in range(2):
+                cols = slice((2 * pair + k) * BLK, (2 * pair + k + 1) * BLK)
+                quantize(se_codes[:, cols], se_scales[:, cols], se_vals[:, k * PACK * BLK:(k + 1) * PACK * BLK])
 
         y = [sb([P, PACK, HALF], F32, f"y{h}") for h in range(2)]
         y_rows = out_0.rearrange("(p r) j -> p r j", r=PACK)
@@ -177,18 +177,19 @@ def tile_attend_fouriermix_pl_kernel(tc, tok, ci, si, ce, se, offs, out_0, out_1
             half = slice(h * HALF, (h + 1) * HALF)
             for r in range(PACK):
                 cols = slice(r * BLK, (r + 1) * BLK)
-                matmul(y_acc[h, r][:], se_codes[:, cols], se_scales[:, cols], b_codes[:, half], b_scales[:, half], False, True)
+                matmul(y_acc[h, r][:], se_codes[:, cols], se_scales[:, cols], mixed_codes["si", h][:], b_scales[:, half], False, True)
                 if h == 0 and r % 2 == 1:
                     nc.vector.tensor_copy(y[h][:, r, :], y_acc[h, r][:])
                 else:
                     nc.scalar.copy(y[h][:, r, :], y_acc[h, r][:])
-                if r % 2 == 1:
+                if h == 0 and r % 2 == 1:
                     nc.sync.dma_start(y_rows[:, r - 1:r + 1, half], y[h][:, r - 1:r + 1, :])
             if h == 0:
                 weave(nc.vector.tensor_copy, 0, HALF)
                 quantize_result(0, HALF)
                 nc.sync.dma_start(words[:, half], y_codes[:, half].bitcast(I32))
             else:
+                nc.sync.dma_start(y_rows[:, :, half], y[h][:])
                 weave(nc.vector.tensor_copy, HALF, HALF + BLK)
                 weave(nc.scalar.copy, HALF + BLK, J)
                 quantize_result(HALF, HALF + BLK)

@@ -91,16 +91,21 @@ def tile_attend_fouriermix_pl_kernel(tc, tok, ci, si, ce, se, offs, out_0, out_1
 
         moving = {}
 
-        def prepare(name, h, engine_copy):
-            staged = sb([P, PACK * HALF], BF16, f"{name}_vals{h}")
+        staged = {}
+
+        def interleave(name, b0, b1, engine_copy):
+            staged[name, b0] = sb([P, PACK * (b1 - b0) * BLK], BF16, f"{name}_vals{b0}")
             engine_copy(
-                staged[:].rearrange("p (c i t) -> p c t i", i=4, t=PACK),
-                raw[name][:, :, h * HALF:(h + 1) * HALF].rearrange("p t (c i) -> p c t i", i=4))
-            w_codes = sb([P, HALF], U32, f"{name}_codes{h}")
-            w_scales = sb([P, HALF], U8, f"{name}_scales{h}")
-            quantize(w_codes[:], w_scales[:], staged[:])
-            for k in range(2):
-                moving[name, 2 * h + k] = (w_codes[:, k * BLK:(k + 1) * BLK], w_scales[:, k * BLK:(k + 1) * BLK])
+                staged[name, b0][:].rearrange("p (c i t) -> p c t i", i=4, t=PACK),
+                raw[name][:, :, b0 * BLK:b1 * BLK].rearrange("p t (c i) -> p c t i", i=4))
+
+        def quantize_moving(name, b0, b1):
+            w_codes = sb([P, (b1 - b0) * BLK], U32, f"{name}_codes{b0}")
+            w_scales = sb([P, (b1 - b0) * BLK], U8, f"{name}_scales{b0}")
+            quantize(w_codes[:], w_scales[:], staged[name, b0][:])
+            for b in range(b0, b1):
+                cols = slice((b - b0) * BLK, (b - b0 + 1) * BLK)
+                moving[name, b] = (w_codes[:, cols], w_scales[:, cols])
 
         def first_stage(name, h):
             vals = mixed[name][0]
@@ -116,13 +121,18 @@ def tile_attend_fouriermix_pl_kernel(tc, tok, ci, si, ce, se, offs, out_0, out_1
 
         a_scales = mixed["ci"][1]
         b_scales = mixed["si"][1]
-        prepare("ci", 0, nc.vector.tensor_copy)
+        interleave("ci", 0, 1, nc.vector.tensor_copy)
+        interleave("ci", 1, 2, nc.vector.tensor_copy)
+        quantize_moving("ci", 0, 1)
         quantize_tokens(3, 4, "ci_vals0")
-        prepare("ci", 1, nc.scalar.copy)
+        quantize_moving("ci", 1, 2)
+        interleave("ci", 2, 4, nc.scalar.copy)
+        quantize_moving("ci", 2, 4)
         first_stage("ci", 0)
         first_stage("ci", 1)
-        prepare("si", 0, nc.vector.tensor_copy)
-        prepare("si", 1, nc.vector.tensor_copy)
+        for b0 in (0, 2):
+            interleave("si", b0, b0 + 2, nc.vector.tensor_copy)
+            quantize_moving("si", b0, b0 + 2)
         first_stage("si", 0)
         first_stage("si", 1)
         quantize_mixed("ci", 0, "si_vals0")

from contextlib import ExitStack

import concourse.mybir as mybir
from concourse.masks import make_identity

E, T, I, J, F = 512, 2048, 512, 512, 512
FLOPS = 4 * 2 * 512 * 512 * 512

F32 = mybir.dt.float32
BF16 = mybir.dt.bfloat16
I32 = mybir.dt.int32
U32 = mybir.dt.uint32
U16 = mybir.dt.uint16
U8 = mybir.dt.uint8
FP8X4 = mybir.dt.float8_e4m3fn_x4

P = 128
PACK = 4
BLK = 128
HALF = 256


def tile_attend_fouriermix_pl_kernel(tc, tok, ci, si, ce, se, offs, out_0, out_1, out_2):
    nc = tc.nc
    with ExitStack() as ctx:
        keep = ctx.enter_context(tc.tile_pool(name="keep", bufs=1))
        psum = ctx.enter_context(tc.psum_pool(name="psum", bufs=1))

        def sb(shape, dtype, name, tag=None):
            return keep.tile(shape, dtype, name=name, tag=tag or name, align_bytes=64)

        def bank(b, shape, name):
            return psum.tile(shape, F32, name=name, tag=f"bank{b}")

        def quantize(codes, scales, values):
            nc.vector.quantize_mx(out=codes.bitcast(FP8X4), scales=scales, in_=values)

        def matmul(out, w_codes, w_scales, m_codes, m_scales, start, stop):
            nc.tensor.matmul_mx(out=out, lhsT=w_codes.bitcast(FP8X4), lhsT_scale=w_scales,
                                rhs=m_codes.bitcast(FP8X4), rhs_scale=m_scales, start=start, stop=stop)

        offsets = keep.tile([P, I // 16], U16, name="offsets")
        tok_rows = tok.rearrange("(m t) c -> m t c", t=PACK)
        planes = [sb([P, T], F32, f"tok{t}") for t in range(PACK)]
        nc.sync.dma_start(planes[0][:], tok_rows[:, 0, :])
        nc.sync.dma_start(offsets[:], offs)
        for t in range(1, PACK):
            nc.sync.dma_start(planes[t][:], tok_rows[:, t, :])
        raw = {}
        for name, src in (("ci", ci), ("si", si), ("ce", ce), ("se", se)):
            raw[name] = sb([P, PACK, 512], F32, f"raw_{name}")
            nc.sync.dma_start(raw[name][:], src.rearrange("(p t) c -> p t c", t=PACK))

        ident = sb([P, P], F32, "ident")
        make_identity(nc, ident[:])

        x_vals = sb([P, PACK * I], BF16, "x_vals")
        x_codes = {}
        x_scales = sb([P, E], U8, "x_scales")

        def quantize_tokens(t0, t1, tag):
            codes = sb([P, (t1 - t0) * BLK], U32, f"x_codes{t0}", tag)
            quantize(codes[:], x_scales[:, t0 * BLK:t1 * BLK], x_vals[:, t0 * I:t1 * I])
            for t in range(t0, t1):
                x_codes[t] = codes[:, (t - t0) * BLK:(t - t0 + 1) * BLK]

        for t in range(PACK):
            picked = sb([P, I], BF16, f"picked{t}")
            nc.vector.tensor_copy(picked[:], planes[t][:].indirect(offsets[:]))
            pairs = picked[:].bitcast(F32)
            turned = bank(6 + t % 2, [P, 2, P], f"turned{t}")
            for u in range(2):
                nc.tensor.transpose(turned[:, u, :], pairs[:, u:I // 2:2], ident[:])
            nc.scalar.copy(x_vals[:, t * I:(t + 1) * I].bitcast(F32).rearrange("p (m u) -> p m u", u=2),
                           turned[:].rearrange("p u m -> p m u"))
            if t == 1:
                quantize_tokens(0, 2, None)

        quantize_tokens(2, 3, "tok3")

        mixed = {}
        for name in ("ci", "si"):
            mixed[name] = (sb([P, PACK * J], BF16, f"{name}_out_vals"), sb([P, J], U8, f"{name}_out_scales"))
        mixed_codes = {}

        def quantize_mixed(name, h, tag):
            vals, scales = mixed[name]
            mixed_codes[name, h] = sb([P, HALF], U32, f"{name}_out_codes{h}", tag)
            quantize(mixed_codes[name, h][:], scales[:, h * HALF:(h + 1) * HALF],
                     vals[:, h * PACK * HALF:(h + 1) * PACK * HALF])

        moving = {}

        staged = {}

        def interleave(name, b0, b1, engine_copy):
            staged[name, b0] = sb([P, PACK * (b1 - b0) * BLK], BF16, f"{name}_vals{b0}")
            engine_copy(
                staged[name, b0][:].rearrange("p (c i t) -> p c t i", i=4, t=PACK),
                raw[name][:, :, b0 * BLK:b1 * BLK].rearrange("p t (c i) -> p c t i", i=4))

        def quantize_moving(name, b0, b1):
            w_codes = sb([P, (b1 - b0) * BLK], U32, f"{name}_codes{b0}")
            w_scales = sb([P, (b1 - b0) * BLK], U8, f"{name}_scales{b0}")
            quantize(w_codes[:], w_scales[:], staged[name, b0][:])
            for b in range(b0, b1):
                cols = slice((b - b0) * BLK, (b - b0 + 1) * BLK)
                moving[name, b] = (w_codes[:, cols], w_scales[:, cols])

        def first_stage(name, h):
            vals = mixed[name][0]
            for b in (2 * h, 2 * h + 1):
                w_codes, w_scales = moving[name, b]
                acc = bank((0 if name == "ci" else PACK) + b, [P, PACK, BLK], f"{name}_acc{b}")
                for t in range(PACK):
                    cols = slice(t * BLK, (t + 1) * BLK)
                    matmul(acc[:, t, :], x_codes[t], x_scales[:, cols], w_codes, w_scales, True, True)
                nc.scalar.copy(
                    vals[:, b * PACK * BLK:(b + 1) * PACK * BLK].rearrange("p (j t) -> p j t", t=PACK),
                    acc[:].rearrange("p t j -> p j t"))

        a_scales = mixed["ci"][1]
        b_scales = mixed["si"][1]
        interleave("ci", 0, 1, nc.vector.tensor_copy)
        interleave("ci", 1, 2, nc.vector.tensor_copy)
        quantize_moving("ci", 0, 1)
        quantize_tokens(3, 4, "ci_vals0")
        quantize_moving("ci", 1, 2)
        interleave("ci", 2, 4, nc.scalar.copy)
        quantize_moving("ci", 2, 4)
        first_stage("ci", 0)
        first_stage("ci", 1)
        for b0 in (0, 2):
            interleave("si", b0, b0 + 2, nc.vector.tensor_copy)
            quantize_moving("si", b0, b0 + 2)
        first_stage("si", 0)
        first_stage("si", 1)
        quantize_mixed("ci", 0, "si_vals0")

        ce_vals = sb([P, PACK * F], BF16, "ce_vals")
        ce_codes = sb([P, F], U32, "ce_codes")
        ce_scales = sb([P, F], U8, "ce_scales")
        nc.vector.tensor_copy(ce_vals[:].rearrange("p (r m t) -> p m t r", r=PACK, t=PACK),
                              raw["ce"][:].rearrange("p t (m r) -> p m t r", r=PACK))
        quantize_mixed("ci", 1, "raw_ce")
        quantize(ce_codes[:], ce_scales[:], ce_vals[:])
        quantize_mixed("si", 0, "ce_vals")

        y_acc = {}
        for h in range(2):
            half = slice(h * HALF, (h + 1) * HALF)
            for r in range(PACK):
                cols = slice(r * BLK, (r + 1) * BLK)
                y_acc[h, r] = bank(PACK * h + r, [P, HALF], f"y_acc{h}{r}")
                matmul(y_acc[h, r][:], ce_codes[:, cols], ce_scales[:, cols], mixed_codes["ci", h][:], a_scales[:, half], True, False)

        se_codes = sb([P, F], U32, "se_codes")
        se_scales = sb([P, F], U8, "se_scales")
        for pair, engine_copy in ((0, nc.vector.tensor_copy), (1, nc.scalar.copy)):
            se_vals = sb([P, 2 * BLK * PACK], BF16, f"se_vals{pair}")
            engine_copy(
                se_vals[:].rearrange("p (r m t) -> p m t r", r=2, t=PACK),
                raw["se"][:].rearrange("p t (m r) -> p m t r", r=PACK)[:, :, :, 2 * pair:2 * pair + 2])
            if pair == 1:
                quantize_mixed("si", 1, "se_vals0")
            for k in range(2):
                cols = slice((2 * pair + k) * BLK, (2 * pair + k + 1) * BLK)
                quantize(se_codes[:, cols], se_scales[:, cols], se_vals[:, k * PACK * BLK:(k + 1) * PACK * BLK])

        y = [sb([P, PACK, HALF], F32, f"y{h}") for h in range(2)]
        y_rows = out_0.rearrange("(p r) j -> p r j", r=PACK)
        y_vals = sb([P, PACK * J], BF16, "y_vals")
        y_codes = sb([P, J], U32, "y_codes")
        y_scales = sb([P, J], U8, "y_scales")
        words = out_1[0].rearrange("l c r -> l (c r)").bitcast(I32)

        def weave(engine_copy, j0, j1):
            h = j0 // HALF
            engine_copy(
                y_vals[:, PACK * j0:PACK * j1].rearrange("p (c i r) -> p c r i", i=4, r=PACK),
                y[h][:, :, j0 - h * HALF:j1 - h * HALF].rearrange("p r (c i) -> p c r i", i=4))

        def quantize_result(j0, j1):
            quantize(y_codes[:, j0:j1], y_scales[:, j0:j1], y_vals[:, PACK * j0:PACK * j1])

        for h in range(2):
            half = slice(h * HALF, (h + 1) * HALF)
            for r in range(PACK):
                cols = slice(r * BLK, (r + 1) * BLK)
                matmul(y_acc[h, r][:], se_codes[:, cols], se_scales[:, cols], mixed_codes["si", h][:], b_scales[:, half], False, True)
                if h == 0 and r % 2 == 1:
                    nc.vector.tensor_copy(y[h][:, r, :], y_acc[h, r][:])
                else:
                    nc.scalar.copy(y[h][:, r, :], y_acc[h, r][:])
                if h == 0 and r % 2 == 1:
                    nc.sync.dma_start(y_rows[:, r - 1:r + 1, half], y[h][:, r - 1:r + 1, :])
            if h == 0:
                weave(nc.vector.tensor_copy, 0, HALF)
                quantize_result(0, HALF)
                nc.sync.dma_start(words[:, half], y_codes[:, half].bitcast(I32))
            else:
                nc.sync.dma_start(y_rows[:, :, half], y[h][:])
                weave(nc.vector.tensor_copy, HALF, HALF + BLK)
                weave(nc.scalar.copy, HALF + BLK, J)
                quantize_result(HALF, HALF + BLK)
                quantize_result(HALF + BLK, J)
                nc.sync.dma_start(words[:, half], y_codes[:, half].bitcast(I32))
        scale_rows = out_2[0].bitcast(I32)
        for q in range(4):
            queue = nc.scalar if q % 2 == 0 else nc.sync
            queue.dma_start(scale_rows[4 * q:4 * q + 4, :], y_scales[32 * q:32 * q + 4, :].bitcast(I32))
